import numpy as np
import ml_dtypes


def mxq(x, axis, fmt="e4m3"):
    dtype, down = {"e4m3": (ml_dtypes.float8_e4m3fn, 7), "e5m2": (ml_dtypes.float8_e5m2, 14)}[fmt]
    v = np.moveaxis(np.asarray(x, np.float32).astype(ml_dtypes.bfloat16).astype(np.float64), axis, -1)
    blocks = v.reshape(v.shape[:-1] + (-1, 32))
    amax = np.abs(blocks).max(-1, keepdims=True)
    byte = np.maximum(np.where(amax > 0, np.frexp(amax)[1] - 1 + 127, 0) - down, 1)
    scale = np.exp2(byte - 127.0)
    codes = (blocks / scale).astype(np.float32).astype(dtype).astype(np.float64)
    return np.moveaxis((codes * scale).reshape(v.shape), -1, axis)


WIDE = False


def mx_kscale(k):
    if not WIDE:
        return np.ones(k)
    levels = np.array([10, -10, 5, -5, 0])
    if k % 512:
        return np.exp2(np.random.permutation(np.resize(levels, k // 32))).repeat(32)
    a = np.empty((k // 512, 16))
    for p in range(k // 512):
        a[p, :8] = np.random.permutation(np.resize(levels, 8))
        for g in range(8):
            far = levels[np.abs(levels - a[p, g]) >= 10]
            a[p, g + 8] = far[np.random.randint(len(far))]
    return np.exp2(a.ravel()).repeat(32)


def f64(x):
    return np.asarray(x).astype(np.float64)


def striped(idx):
    return np.tile(idx.reshape(-1, 16).T, (8, 1)).astype(np.uint16)


def unstriped(offs):
    return offs[:16].T.reshape(-1).astype(np.int64)


E2M1 = np.array([0.0, 0.5, 1.0, 1.5, 2.0, 3.0, 4.0, 6.0, -0.0, -0.5, -1.0, -1.5, -2.0, -3.0, -4.0, -6.0])


def pack_weight(w, fmt):
    k, n = w.shape
    w = f64(np.asarray(w, np.float32).astype(ml_dtypes.bfloat16)).reshape(k // 32, 32, n)
    amax = np.abs(w).max(1)
    if fmt == "e4m3":
        byte = np.frexp(amax)[1] - 1 + 127 - 7
    else:
        mant, ex = np.frexp(amax / 6.0)
        byte = np.where(mant > 0.5, ex, ex - 1) + 127
    byte = np.clip(np.where(amax > 0, byte, 1), 1, 254)
    scaled = (w * np.exp2(127.0 - byte)[:, None, :]).reshape(k, n).astype(np.float32)
    by_word = np.ascontiguousarray(scaled.reshape(k // 512, 128, 4, n).transpose(0, 1, 3, 2))
    if fmt == "e4m3":
        words = by_word.astype(ml_dtypes.float8_e4m3fn).view(np.uint8)
    else:
        c = by_word.astype(ml_dtypes.float4_e2m1fn).view(np.uint8) & 0xF
        words = (c[..., 0::2] | (c[..., 1::2] << 4)).reshape(k // 512, 128, 2 * n)
    return np.ascontiguousarray(words), np.ascontiguousarray(byte.astype(np.uint8).reshape(k // 512, 16, n))


def unpack_weight(words, scales, fmt):
    g, _, n = scales.shape
    words = np.ascontiguousarray(words).reshape(g, 128, n, -1)
    if fmt == "e4m3":
        vals = words.view(ml_dtypes.float8_e4m3fn).astype(np.float64)
    else:
        nib = np.empty((g, 128, n, 4), np.uint8)
        nib[..., 0::2] = words & 0xF
        nib[..., 1::2] = words >> 4
        vals = E2M1[nib]
    vals = vals * np.repeat(np.exp2(scales.astype(np.float64) - 127.0), 8, axis=1)[..., None]
    return vals.transpose(0, 1, 3, 2).reshape(g * 512, n)


def silu(v):
    return v / (1.0 + np.exp(-np.maximum(v, -700.0)))


K, T, S, H, N = 512, 1024, 512, 512, 256


def setup_inputs():
    n = np.random.standard_normal
    s = mx_kscale(K)
    u = mx_kscale(H)
    hard = np.random.permutation(T)[:S]
    x = pack_weight(n((K, T)) * s[:, None], "e4m3")
    w = pack_weight(n((K, N)) / np.sqrt(K) / s[:, None], "e4m3")
    w1 = pack_weight(n((K, H)) / np.sqrt(K) / s[:, None] * u, "e4m3")
    w2 = pack_weight(n((H, N)) / np.sqrt(H) / u[:, None], "e4m3")
    return {
        "x_words": x[0],
        "x_scales": x[1],
        "w_words": w[0],
        "w_scales": w[1],
        "w1_words": w1[0],
        "w1_scales": w1[1],
        "w2_words": w2[0],
        "w2_scales": w2[1],
        "offs": striped(hard),
    }


def reference(x_words, x_scales, w_words, w_scales, w1_words, w1_scales, w2_words, w2_scales, offs):
    w = unpack_weight(w_words, w_scales, "e4m3")
    w1 = unpack_weight(w1_words, w1_scales, "e4m3")
    w2 = unpack_weight(w2_words, w2_scales, "e4m3")
    idx = unstriped(offs)
    x = unpack_weight(x_words, x_scales, "e4m3")
    out = w.T @ x
    h = silu(w1.T @ x[:, idx])
    out[:, idx] = w2.T @ mxq(h, 0, "e4m3")
    return out

@@ -1,0 +1,170 @@
+from contextlib import ExitStack
+
+import concourse.mybir as mybir
+
+K, T, S, H, N = 512, 1024, 512, 512, 256
+FLOPS = 2 * K * N * T + 2 * K * H * S + 2 * H * N * S
+
+F32 = mybir.dt.float32
+BF16 = mybir.dt.bfloat16
+I32 = mybir.dt.int32
+U32 = mybir.dt.uint32
+U16 = mybir.dt.uint16
+U8 = mybir.dt.uint8
+FP8X4 = mybir.dt.float8_e4m3fn_x4
+SILU = mybir.ActivationFunctionType.Silu
+
+P = 128
+PACK = 4
+CHUNK = 128
+CHUNKS = S // CHUNK
+BANK = 512
+LIST_ROWS = 16
+
+
+def tile_moe_cas_mlp_silu_kernel(
+    tc, x_words, x_scales, w_words, w_scales, w1_words, w1_scales, w2_words, w2_scales, offs, out
+):
+    nc = tc.nc
+    with ExitStack() as ctx:
+        keep = ctx.enter_context(tc.tile_pool(name="keep", bufs=1))
+        psum = ctx.enter_context(tc.psum_pool(name="psum", bufs=1))
+
+        offsets = keep.tile([P, S // LIST_ROWS], U16, name="offsets")
+        x_w = keep.tile([P, T], U32, name="x_w", align_bytes=64)
+        x_s = keep.tile([P, T], U8, name="x_s", align_bytes=64)
+        w_w = keep.tile([P, N], U32, name="w_w", align_bytes=64)
+        w_s = keep.tile([P, N], U8, name="w_s", align_bytes=64)
+        w1_raw_w = keep.tile([P, H], U32, name="w1_raw_w", align_bytes=64)
+        w1_raw_s = keep.tile([P, H], U8, name="w1_raw_s", align_bytes=64)
+        w1_w = keep.tile([P, H], U32, name="w1_w", align_bytes=64)
+        w1_s = keep.tile([P, H], U8, name="w1_s", align_bytes=64)
+        w2_w = keep.tile([P, N], U32, name="w2_w", align_bytes=64)
+        w2_s = keep.tile([P, N], U8, name="w2_s", align_bytes=64)
+        g_w = keep.tile([P, S], U32, name="g_w", align_bytes=64)
+        g_s = keep.tile([P, S], U8, name="g_s", align_bytes=64)
+        h_bf = keep.tile([P, S, PACK], BF16, name="h_bf", align_bytes=64)
+        h_w = keep.tile([P, S], U32, name="h_w", align_bytes=64)
+        h_s = keep.tile([P, S], U8, name="h_s", align_bytes=64)
+        z = [keep.tile([P, S], F32, name="z%d" % r, align_bytes=64) for r in range(2)]
+        y = [keep.tile([P, T], F32, name="y%d" % r, align_bytes=64) for r in range(2)]
+        warm_in = keep.tile([P, 8], F32, name="warm_in")
+        warm_out = keep.tile([P, 8], F32, name="warm_out")
+
+        def load_words(queue, tile, words):
+            queue.dma_start(tile[:].bitcast(I32), words[0].rearrange("p n d -> p (n d)").bitcast(I32))
+
+        def load_scales(queue, tile, scales, quadrant):
+            queue.dma_start(
+                tile[32 * quadrant : 32 * quadrant + 4, :].bitcast(I32),
+                scales[0, 4 * quadrant : 4 * quadrant + 4, :].bitcast(I32),
+            )
+
+        def mx(dst, lw, ls, rw, rs):
+            nc.tensor.matmul_mx(
+                out=dst, lhsT=lw.bitcast(FP8X4), lhsT_scale=ls, rhs=rw.bitcast(FP8X4), rhs_scale=rs,
+                start=True, stop=True,
+            )
+
+        def entries(first, count):
+            return offsets[:, first // LIST_ROWS : (first + count) // LIST_ROWS]
+
+        nc.vector.memset(x_s[:].bitcast(I32), 0)
+        nc.vector.memset(w1_raw_s[:].bitcast(I32), 0)
+        nc.gpsimd.memset(w2_s[:].bitcast(I32), 0)
+        nc.vector.memset(w_s[:].bitcast(I32), 0)
+        nc.vector.memset(warm_in[:], 0.0)
+
+        nc.sync.dma_start(offsets[:], offs)
+        load_words(nc.sync, x_w, x_words)
+        for q in range(4):
+            load_scales(nc.scalar, x_s, x_scales, q)
+        load_scales(nc.scalar, w1_raw_s, w1_scales, 0)
+        load_words(nc.sync, w1_raw_w, w1_words)
+        load_scales(nc.scalar, w1_raw_s, w1_scales, 1)
+        load_scales(nc.gpsimd, w1_raw_s, w1_scales, 3)
+        nc.scalar.activation(warm_out[:], warm_in[:], SILU)
+        load_words(nc.scalar, w2_w, w2_words)
+        load_scales(nc.sync, w1_raw_s, w1_scales, 2)
+        load_words(nc.sync, w_w, w_words)
+        for q in range(4):
+            load_scales(nc.sync, w_s, w_scales, q)
+        load_scales(nc.sync, w2_s, w2_scales, 0)
+        for q in range(1, 4):
+            load_scales(nc.gpsimd, w2_s, w2_scales, q)
+
+        def gather(first, count):
+            cols = slice(first, first + count)
+            nc.vector.tensor_copy(g_w[:, cols], x_w[:].indirect(entries(first, count)))
+            nc.vector.tensor_copy(g_s[:, cols], x_s[:].indirect(entries(first, count)))
+
+        def first_layer(c):
+            cols = slice(c * CHUNK, (c + 1) * CHUNK)
+            acc = psum.tile([P, PACK, CHUNK], F32, name="acc_h", tag="acc_h", bufs=3)
+            for d in range(PACK):
+                m = slice(d * P, (d + 1) * P)
+                mx(acc[:, d, :], w1_w[:, m], w1_s[:, m], g_w[:, cols], g_s[:, cols])
+            nc.scalar.activation(h_bf[:, cols, :], acc[:].rearrange("p d j -> p j d"), SILU)
+
+        def quantise(c):
+            cols = slice(c * CHUNK, (c + 1) * CHUNK)
+            nc.vector.quantize_mx(
+                out=h_w[:, cols].bitcast(FP8X4), scales=h_s[:, cols],
+                in_=h_bf[:, cols, :].rearrange("p j d -> p (j d)"),
+            )
+
+        def second_layer(r, first, count, tag, bufs):
+            cols = slice(first, first + count)
+            m = slice(r * P, (r + 1) * P)
+            acc = psum.tile([P, count], F32, name=tag, tag=tag, bufs=bufs)
+            mx(acc[:], w2_w[:, m], w2_s[:, m], h_w[:, cols], h_s[:, cols])
+            nc.scalar.copy(z[r][:, cols], acc[:])
+
+        def light(r, b, on_vector):
+            cols = slice(b * BANK, (b + 1) * BANK)
+            m = slice(r * P, (r + 1) * P)
+            acc = psum.tile([P, BANK], F32, name="acc_y", tag="acc_y", bufs=2)
+            mx(acc[:], w_w[:, m], w_s[:, m], x_w[:, cols], x_s[:, cols])
+            if on_vector:
+                nc.vector.tensor_copy(y[r][:, cols], acc[:])
+            else:
+                nc.scalar.copy(y[r][:, cols], acc[:])
+
+        def scatter(r, first, count):
+            nc.vector.tensor_copy(y[r][:].indirect(entries(first, count)), z[r][:, first : first + count])
+
+        gather(0, CHUNK)
+        nc.vector.tensor_copy(
+            w1_w[:].bitcast(I32).rearrange("p (d c i) -> p c d i", d=PACK, i=4),
+            w1_raw_w[:].bitcast(I32).rearrange("p (c i d) -> p c d i", d=PACK, i=4),
+        )
+        nc.vector.tensor_copy(
+            w1_s[:].rearrange("p (d c i) -> p c d i", d=PACK, i=16),
+            w1_raw_s[:].rearrange("p (c i d) -> p c d i", d=PACK, i=16),
+        )
+        first_layer(0)
+        gather(CHUNK, CHUNK)
+        light(0, 0, False)
+        first_layer(1)
+        quantise(0)
+        second_layer(0, 0, CHUNK, "acc_z0", 2)
+        gather(2 * CHUNK, 2 * CHUNK)
+        light(0, 1, True)
+        quantise(1)
+        first_layer(2)
+        scatter(0, 0, CHUNK)
+        second_layer(0, CHUNK, CHUNK, "acc_z0", 2)
+        first_layer(3)
+        quantise(2)
+        scatter(0, CHUNK, CHUNK)
+        second_layer(0, 2 * CHUNK, CHUNK, "acc_z0", 2)
+        quantise(3)
+        scatter(0, 2 * CHUNK, CHUNK)
+        second_layer(0, 3 * CHUNK, CHUNK, "acc_z0", 2)
+        scatter(0, 3 * CHUNK, CHUNK)
+        nc.sync.dma_start(out[0:P, :], y[0][:])
+        light(1, 0, False)
+        light(1, 1, False)
+        second_layer(1, 0, S, "acc_z1", 1)
+        scatter(1, 0, S)
+        nc.sync.dma_start(out[P : 2 * P, :], y[1][:])

@@ -39,14 +39,14 @@ def tile_moe_cas_mlp_silu_kernel(
         w1_raw_s = keep.tile([P, H], U8, name="w1_raw_s", align_bytes=64)
         w1_w = keep.tile([P, H], U32, name="w1_w", align_bytes=64)
         w1_s = keep.tile([P, H], U8, name="w1_s", align_bytes=64)
-        w2_w = keep.tile([P, N], U32, name="w2_w", align_bytes=64)
-        w2_s = keep.tile([P, N], U8, name="w2_s", align_bytes=64)
+        w2_w = w1_raw_w[:, 0:N]
+        w2_s = w1_raw_w[:, N : N + N // PACK].bitcast(U8)
         g_w = keep.tile([P, S], U32, name="g_w", align_bytes=64)
         g_s = keep.tile([P, S], U8, name="g_s", align_bytes=64)
         h_bf = keep.tile([P, S, PACK], BF16, name="h_bf", align_bytes=64)
-        h_w = keep.tile([P, S], U32, name="h_w", align_bytes=64)
-        h_s = keep.tile([P, S], U8, name="h_s", align_bytes=64)
-        z = [keep.tile([P, S], F32, name="z%d" % r, align_bytes=64) for r in range(2)]
+        h_w = [keep.tile([P, CHUNK], U32, name="h_w%d" % i, align_bytes=64) for i in range(2)]
+        h_s = [keep.tile([P, CHUNK], U8, name="h_s%d" % i, align_bytes=64) for i in range(2)]
+        z = keep.tile([P, 2, S], F32, name="z", align_bytes=64)
         y = [keep.tile([P, T], F32, name="y%d" % r, align_bytes=64) for r in range(2)]
         warm_in = keep.tile([P, 8], F32, name="warm_in")
         warm_out = keep.tile([P, 8], F32, name="warm_out")
@@ -69,102 +69,113 @@ def tile_moe_cas_mlp_silu_kernel(
         def entries(first, count):
             return offsets[:, first // LIST_ROWS : (first + count) // LIST_ROWS]
 
+        def load_scales_filled(queue, tile, scales, quadrant):
+            rows = scales[0, 4 * quadrant : 4 * quadrant + 4, :].bitcast(I32)
+            queue.dma_start(
+                tile[32 * quadrant : 32 * quadrant + 32, :].bitcast(I32),
+                rows.unsqueeze(0).broadcast_to([8, 4, rows.shape[1]]),
+            )
+
         nc.vector.memset(x_s[:].bitcast(I32), 0)
-        nc.vector.memset(w1_raw_s[:].bitcast(I32), 0)
-        nc.gpsimd.memset(w2_s[:].bitcast(I32), 0)
-        nc.vector.memset(w_s[:].bitcast(I32), 0)
+        nc.vector.memset(w1_raw_s[0:64, :].bitcast(I32), 0)
+        nc.vector.memset(w1_raw_s[64:96, :].bitcast(I32), 0)
+        nc.vector.memset(w_s[0:64, :].bitcast(I32), 0)
         nc.vector.memset(warm_in[:], 0.0)
+        nc.scalar.activation(warm_out[:], warm_in[:], SILU)
 
         nc.sync.dma_start(offsets[:], offs)
-        load_words(nc.sync, x_w, x_words)
         for q in range(4):
-            load_scales(nc.scalar, x_s, x_scales, q)
-        load_scales(nc.scalar, w1_raw_s, w1_scales, 0)
+            load_scales(nc.sync, x_s, x_scales, q)
         load_words(nc.sync, w1_raw_w, w1_words)
-        load_scales(nc.scalar, w1_raw_s, w1_scales, 1)
-        load_scales(nc.gpsimd, w1_raw_s, w1_scales, 3)
-        nc.scalar.activation(warm_out[:], warm_in[:], SILU)
-        load_words(nc.scalar, w2_w, w2_words)
-        load_scales(nc.sync, w1_raw_s, w1_scales, 2)
+        load_words(nc.sync, x_w, x_words)
+        for q in range(3):
+            load_scales(nc.sync, w1_raw_s, w1_scales, q)
+        load_scales_filled(nc.gpsimd, w1_raw_s, w1_scales, 3)
         load_words(nc.sync, w_w, w_words)
-        for q in range(4):
+        for q in range(2):
             load_scales(nc.sync, w_s, w_scales, q)
-        load_scales(nc.sync, w2_s, w2_scales, 0)
-        for q in range(1, 4):
-            load_scales(nc.gpsimd, w2_s, w2_scales, q)
+        for q in range(2, 4):
+            load_scales_filled(nc.gpsimd, w_s, w_scales, q)
 
-        def gather(first, count):
-            cols = slice(first, first + count)
-            nc.vector.tensor_copy(g_w[:, cols], x_w[:].indirect(entries(first, count)))
-            nc.vector.tensor_copy(g_s[:, cols], x_s[:].indirect(entries(first, count)))
+        banks = [psum.tile([P, BANK], F32, name="bank%d" % b) for b in range(5)]
 
-        def first_layer(c):
+        def gather_words(first, count):
+            nc.vector.tensor_copy(g_w[:, first : first + count], x_w[:].indirect(entries(first, count)))
+
+        def gather_scales(first, count):
+            nc.vector.tensor_copy(g_s[:, first : first + count], x_s[:].indirect(entries(first, count)))
+
+        def first_layer(c, bank):
             cols = slice(c * CHUNK, (c + 1) * CHUNK)
-            acc = psum.tile([P, PACK, CHUNK], F32, name="acc_h", tag="acc_h", bufs=3)
             for d in range(PACK):
                 m = slice(d * P, (d + 1) * P)
-                mx(acc[:, d, :], w1_w[:, m], w1_s[:, m], g_w[:, cols], g_s[:, cols])
-            nc.scalar.activation(h_bf[:, cols, :], acc[:].rearrange("p d j -> p j d"), SILU)
+                mx(bank[:, m], w1_w[:, m], w1_s[:, m], g_w[:, cols], g_s[:, cols])
+            nc.scalar.activation(h_bf[:, cols, :], bank[:].rearrange("p (d j) -> p j d", d=PACK), SILU)
 
         def quantise(c):
             cols = slice(c * CHUNK, (c + 1) * CHUNK)
             nc.vector.quantize_mx(
-                out=h_w[:, cols].bitcast(FP8X4), scales=h_s[:, cols],
+                out=h_w[c % 2][:].bitcast(FP8X4), scales=h_s[c % 2][:],
                 in_=h_bf[:, cols, :].rearrange("p j d -> p (j d)"),
             )
 
-        def second_layer(r, first, count, tag, bufs):
-            cols = slice(first, first + count)
-            m = slice(r * P, (r + 1) * P)
-            acc = psum.tile([P, count], F32, name=tag, tag=tag, bufs=bufs)
-            mx(acc[:], w2_w[:, m], w2_s[:, m], h_w[:, cols], h_s[:, cols])
-            nc.scalar.copy(z[r][:, cols], acc[:])
+        def second_layer(c, bank, copy):
+            for r in range(2):
+                m = slice(r * P, (r + 1) * P)
+                mx(bank[:, m], w2_w[:, m], w2_s[:, m], h_w[c % 2][:], h_s[c % 2][:])
+            copy(z[:, :, c * CHUNK : (c + 1) * CHUNK], bank[:, 0 : 2 * P].rearrange("p (r j) -> p r j", r=2))
 
-        def light(r, b, on_vector):
+        def light_matmul(r, b, bank):
             cols = slice(b * BANK, (b + 1) * BANK)
             m = slice(r * P, (r + 1) * P)
-            acc = psum.tile([P, BANK], F32, name="acc_y", tag="acc_y", bufs=2)
-            mx(acc[:], w_w[:, m], w_s[:, m], x_w[:, cols], x_s[:, cols])
-            if on_vector:
-                nc.vector.tensor_copy(y[r][:, cols], acc[:])
-            else:
-                nc.scalar.copy(y[r][:, cols], acc[:])
+            mx(bank[:], w_w[:, m], w_s[:, m], x_w[:, cols], x_s[:, cols])
+
+        def light(r, b, bank):
+            light_matmul(r, b, bank)
+            nc.scalar.copy(y[r][:, b * BANK : (b + 1) * BANK], bank[:])
 
         def scatter(r, first, count):
-            nc.vector.tensor_copy(y[r][:].indirect(entries(first, count)), z[r][:, first : first + count])
+            nc.vector.tensor_copy(y[r][:].indirect(entries(first, count)), z[:, r, first : first + count])
 
-        gather(0, CHUNK)
+        gather_scales(0, S)
         nc.vector.tensor_copy(
             w1_w[:].bitcast(I32).rearrange("p (d c i) -> p c d i", d=PACK, i=4),
             w1_raw_w[:].bitcast(I32).rearrange("p (c i d) -> p c d i", d=PACK, i=4),
         )
-        nc.vector.tensor_copy(
-            w1_s[:].rearrange("p (d c i) -> p c d i", d=PACK, i=16),
-            w1_raw_s[:].rearrange("p (c i d) -> p c d i", d=PACK, i=16),
-        )
-        first_layer(0)
-        gather(CHUNK, CHUNK)
-        light(0, 0, False)
-        first_layer(1)
+        load_words(nc.scalar, w2_w, w2_words)
+        for q in range(3):
+            load_scales(nc.scalar, w2_s, w2_scales, q)
+        load_scales(nc.sync, w2_s, w2_scales, 3)
+        gather_words(0, CHUNK)
+        for half in range(2):
+            d = slice(2 * half, 2 * half + 2)
+            nc.gpsimd.tensor_copy(
+                w1_s[:].rearrange("p (d c i) -> p c d i", d=PACK, i=16)[:, :, d, :],
+                w1_raw_s[:].rearrange("p (c i d) -> p c d i", d=PACK, i=16)[:, :, d, :],
+            )
+        first_layer(0, banks[0])
+        gather_words(CHUNK, CHUNK)
+        first_layer(1, banks[1])
+        light(0, 0, banks[2])
         quantise(0)
-        second_layer(0, 0, CHUNK, "acc_z0", 2)
-        gather(2 * CHUNK, 2 * CHUNK)
-        light(0, 1, True)
+        gather_words(2 * CHUNK, 2 * CHUNK)
+        light_matmul(0, 1, banks[0])
+        second_layer(0, banks[4], nc.scalar.copy)
         quantise(1)
-        first_layer(2)
+        nc.vector.tensor_copy(y[0][:, BANK:], banks[0][:])
+        second_layer(1, banks[3], nc.scalar.copy)
+        first_layer(2, banks[1])
         scatter(0, 0, CHUNK)
-        second_layer(0, CHUNK, CHUNK, "acc_z0", 2)
-        first_layer(3)
+        first_layer(3, banks[4])
         quantise(2)
         scatter(0, CHUNK, CHUNK)
-        second_layer(0, 2 * CHUNK, CHUNK, "acc_z0", 2)
+        second_layer(2, banks[0], nc.scalar.copy)
         quantise(3)
+        light(1, 0, banks[1])
         scatter(0, 2 * CHUNK, CHUNK)
-        second_layer(0, 3 * CHUNK, CHUNK, "acc_z0", 2)
+        second_layer(3, banks[3], nc.scalar.copy)
+        light(1, 1, banks[4])
         scatter(0, 3 * CHUNK, CHUNK)
         nc.sync.dma_start(out[0:P, :], y[0][:])
-        light(1, 0, False)
-        light(1, 1, False)
-        second_layer(1, 0, S, "acc_z1", 1)
         scatter(1, 0, S)
         nc.sync.dma_start(out[P : 2 * P, :], y[1][:])

@@ -166,16 +166,16 @@ def tile_moe_cas_mlp_silu_kernel(
         second_layer(1, banks[3], nc.scalar.copy)
         first_layer(2, banks[1])
         scatter(0, 0, CHUNK)
+        scatter(0, CHUNK, CHUNK)
         first_layer(3, banks[4])
         quantise(2)
-        scatter(0, CHUNK, CHUNK)
-        second_layer(2, banks[0], nc.scalar.copy)
         quantise(3)
-        light(1, 0, banks[1])
-        scatter(0, 2 * CHUNK, CHUNK)
-        second_layer(3, banks[3], nc.scalar.copy)
-        light(1, 1, banks[4])
-        scatter(0, 3 * CHUNK, CHUNK)
+        light(1, 0, banks[2])
+        light(1, 1, banks[0])
+        second_layer(2, banks[2], nc.scalar.copy)
+        second_layer(3, banks[0], nc.scalar.copy)
+        scatter(1, 0, 2 * CHUNK)
+        scatter(0, 2 * CHUNK, 2 * CHUNK)
         nc.sync.dma_start(out[0:P, :], y[0][:])
-        scatter(1, 0, S)
+        scatter(1, 2 * CHUNK, 2 * CHUNK)
         nc.sync.dma_start(out[P : 2 * P, :], y[1][:])

@@ -36,12 +36,12 @@ def tile_moe_cas_mlp_silu_kernel(
         w_w = keep.tile([P, N], U32, name="w_w", align_bytes=64)
         w_s = keep.tile([P, N], U8, name="w_s", align_bytes=64)
         w1_raw_w = keep.tile([P, H], U32, name="w1_raw_w", align_bytes=64)
-        w1_raw_s = keep.tile([P, H], U8, name="w1_raw_s", align_bytes=64)
+        w1_raw_s = keep.tile([P, H], U8, name="w1_raw_s", tag="stage", align_bytes=64)
         w1_w = keep.tile([P, H], U32, name="w1_w", align_bytes=64)
         w1_s = keep.tile([P, H], U8, name="w1_s", align_bytes=64)
         w2_w = w1_raw_w[:, 0:N]
         w2_s = w1_raw_w[:, N : N + N // PACK].bitcast(U8)
-        g_w = keep.tile([P, S], U32, name="g_w", align_bytes=64)
+        g_first = keep.tile([P, CHUNK], U32, name="g_first", align_bytes=64)
         g_s = keep.tile([P, S], U8, name="g_s", align_bytes=64)
         h_bf = keep.tile([P, S, PACK], BF16, name="h_bf", align_bytes=64)
         h_w = [keep.tile([P, CHUNK], U32, name="h_w%d" % i, align_bytes=64) for i in range(2)]
@@ -99,17 +99,17 @@ def tile_moe_cas_mlp_silu_kernel(
 
         banks = [psum.tile([P, BANK], F32, name="bank%d" % b) for b in range(5)]
 
-        def gather_words(first, count):
-            nc.vector.tensor_copy(g_w[:, first : first + count], x_w[:].indirect(entries(first, count)))
+        def gather_words(dst, first, count):
+            nc.vector.tensor_copy(dst, x_w[:].indirect(entries(first, count)))
 
         def gather_scales(first, count):
             nc.vector.tensor_copy(g_s[:, first : first + count], x_s[:].indirect(entries(first, count)))
 
-        def first_layer(c, bank):
+        def first_layer(c, words, bank):
             cols = slice(c * CHUNK, (c + 1) * CHUNK)
             for d in range(PACK):
                 m = slice(d * P, (d + 1) * P)
-                mx(bank[:, m], w1_w[:, m], w1_s[:, m], g_w[:, cols], g_s[:, cols])
+                mx(bank[:, m], w1_w[:, m], w1_s[:, m], words, g_s[:, cols])
             nc.scalar.activation(h_bf[:, cols, :], bank[:].rearrange("p (d j) -> p j d", d=PACK), SILU)
 
         def quantise(c):
@@ -146,28 +146,29 @@ def tile_moe_cas_mlp_silu_kernel(
         for q in range(3):
             load_scales(nc.scalar, w2_s, w2_scales, q)
         load_scales(nc.sync, w2_s, w2_scales, 3)
-        gather_words(0, CHUNK)
+        gather_words(g_first[:], 0, CHUNK)
         for half in range(2):
             d = slice(2 * half, 2 * half + 2)
-            nc.gpsimd.tensor_copy(
+            nc.vector.tensor_copy(
                 w1_s[:].rearrange("p (d c i) -> p c d i", d=PACK, i=16)[:, :, d, :],
                 w1_raw_s[:].rearrange("p (c i d) -> p c d i", d=PACK, i=16)[:, :, d, :],
             )
-        first_layer(0, banks[0])
-        gather_words(CHUNK, CHUNK)
-        first_layer(1, banks[1])
+        first_layer(0, g_first[:], banks[0])
+        g_rest = keep.tile([P, S - CHUNK], U32, name="g_rest", tag="stage", align_bytes=64)
+        gather_words(g_rest[:, 0:CHUNK], CHUNK, CHUNK)
+        first_layer(1, g_rest[:, 0:CHUNK], banks[1])
         light(0, 0, banks[2])
         quantise(0)
-        gather_words(2 * CHUNK, 2 * CHUNK)
+        gather_words(g_rest[:, CHUNK:], 2 * CHUNK, 2 * CHUNK)
         light_matmul(0, 1, banks[0])
         second_layer(0, banks[4], nc.scalar.copy)
         quantise(1)
         nc.vector.tensor_copy(y[0][:, BANK:], banks[0][:])
         second_layer(1, banks[3], nc.scalar.copy)
-        first_layer(2, banks[1])
+        first_layer(2, g_rest[:, CHUNK : 2 * CHUNK], banks[1])
         scatter(0, 0, CHUNK)
         scatter(0, CHUNK, CHUNK)
-        first_layer(3, banks[4])
+        first_layer(3, g_rest[:, 2 * CHUNK :], banks[4])
         quantise(2)
         quantise(3)
         light(1, 0, banks[2])

@@ -48,8 +48,6 @@ def tile_moe_cas_mlp_silu_kernel(
         h_s = [keep.tile([P, CHUNK], U8, name="h_s%d" % i, align_bytes=64) for i in range(2)]
         z = keep.tile([P, 2, S], F32, name="z", align_bytes=64)
         y = [keep.tile([P, T], F32, name="y%d" % r, align_bytes=64) for r in range(2)]
-        warm_in = keep.tile([P, 8], F32, name="warm_in")
-        warm_out = keep.tile([P, 8], F32, name="warm_out")
 
         def load_words(queue, tile, words):
             queue.dma_start(tile[:].bitcast(I32), words[0].rearrange("p n d -> p (n d)").bitcast(I32))
@@ -80,8 +78,6 @@ def tile_moe_cas_mlp_silu_kernel(
         nc.vector.memset(w1_raw_s[0:64, :].bitcast(I32), 0)
         nc.vector.memset(w1_raw_s[64:96, :].bitcast(I32), 0)
         nc.vector.memset(w_s[0:64, :].bitcast(I32), 0)
-        nc.vector.memset(warm_in[:], 0.0)
-        nc.scalar.activation(warm_out[:], warm_in[:], SILU)
 
         nc.sync.dma_start(offsets[:], offs)
         for q in range(4):

@@ -17,9 +17,10 @@ SILU = mybir.ActivationFunctionType.Silu
 P = 128
 PACK = 4
 CHUNK = 128
-CHUNKS = S // CHUNK
 BANK = 512
 LIST_ROWS = 16
+PERIOD = 14
+REPEATS = 5
 
 
 def tile_moe_cas_mlp_silu_kernel(
@@ -33,29 +34,47 @@ def tile_moe_cas_mlp_silu_kernel(
         offsets = keep.tile([P, S // LIST_ROWS], U16, name="offsets")
         x_w = keep.tile([P, T], U32, name="x_w", align_bytes=64)
         x_s = keep.tile([P, T], U8, name="x_s", align_bytes=64)
-        w_w = keep.tile([P, N], U32, name="w_w", align_bytes=64)
-        w_s = keep.tile([P, N], U8, name="w_s", align_bytes=64)
         w1_raw_w = keep.tile([P, H], U32, name="w1_raw_w", align_bytes=64)
-        w1_raw_s = keep.tile([P, H], U8, name="w1_raw_s", tag="stage", align_bytes=64)
         w1_w = keep.tile([P, H], U32, name="w1_w", align_bytes=64)
         w1_s = keep.tile([P, H], U8, name="w1_s", align_bytes=64)
-        w2_w = w1_raw_w[:, 0:N]
-        w2_s = w1_raw_w[:, N : N + N // PACK].bitcast(U8)
-        g_first = keep.tile([P, CHUNK], U32, name="g_first", align_bytes=64)
-        g_s = keep.tile([P, S], U8, name="g_s", align_bytes=64)
         h_bf = keep.tile([P, S, PACK], BF16, name="h_bf", align_bytes=64)
-        h_w = [keep.tile([P, CHUNK], U32, name="h_w%d" % i, align_bytes=64) for i in range(2)]
-        h_s = [keep.tile([P, CHUNK], U8, name="h_s%d" % i, align_bytes=64) for i in range(2)]
+        h_w = keep.tile([P, S], U32, name="h_w", align_bytes=64)
+        h_s = keep.tile([P, S], U8, name="h_s", align_bytes=64)
         z = keep.tile([P, 2, S], F32, name="z", align_bytes=64)
         y = [keep.tile([P, T], F32, name="y%d" % r, align_bytes=64) for r in range(2)]
+        banks = [psum.tile([P, BANK], F32, name="bank%d" % b) for b in range(8)]
+        stage = ctx.enter_context(tc.tile_pool(name="stage", bufs=1))
+        w1_raw_s = stage.tile([P, H], U8, name="w1_raw_s", align_bytes=64, offset=1280)
+        w_w = keep.tile([P, N], U32, name="w_w", align_bytes=64)
+        w_s = keep.tile([P, N], U8, name="w_s", align_bytes=64)
+        w2_w = w1_raw_w[:, 0:N]
+        w2_s = w1_raw_w[:, N : N + N // PACK].bitcast(U8)
+        g_w0 = keep.tile([P, CHUNK], U32, name="g_w0", align_bytes=64)
+        g_w = stage.tile([P, 3 * CHUNK], U32, name="g_w", align_bytes=64, offset=0)
+        g_s = keep.tile([P, 3 * CHUNK], U8, name="g_s", align_bytes=64)
+        g_s3 = stage.tile([P, CHUNK], U8, name="g_s3", align_bytes=64, offset=1536)
+        warm = keep.tile([P, 2], F32, name="warm")
 
         def load_words(queue, tile, words):
             queue.dma_start(tile[:].bitcast(I32), words[0].rearrange("p n d -> p (n d)").bitcast(I32))
 
-        def load_scales(queue, tile, scales, quadrant):
+        def load_quadrant(queue, plane, scales, q):
             queue.dma_start(
-                tile[32 * quadrant : 32 * quadrant + 4, :].bitcast(I32),
-                scales[0, 4 * quadrant : 4 * quadrant + 4, :].bitcast(I32),
+                plane[32 * q : 32 * q + 4, :].bitcast(I32), scales[0, 4 * q : 4 * q + 4, :].bitcast(I32)
+            )
+
+        def load_three_quadrants(queue, plane, scales):
+            rows = scales[0, 0:PERIOD, :].bitcast(I32)
+            queue.dma_start(
+                plane[0 : PERIOD * REPEATS, :].bitcast(I32),
+                rows.unsqueeze(0).broadcast_to([REPEATS, PERIOD, rows.shape[1]]),
+            )
+
+        def load_last_quadrant(queue, plane, scales):
+            rows = scales[0, 12:16, :].bitcast(I32)
+            queue.dma_start(
+                plane[96:128, :].bitcast(I32),
+                rows.unsqueeze(0).broadcast_to([8, 4, rows.shape[1]]),
             )
 
         def mx(dst, lw, ls, rw, rs):
@@ -67,112 +86,115 @@ def tile_moe_cas_mlp_silu_kernel(
         def entries(first, count):
             return offsets[:, first // LIST_ROWS : (first + count) // LIST_ROWS]
 
-        def load_scales_filled(queue, tile, scales, quadrant):
-            rows = scales[0, 4 * quadrant : 4 * quadrant + 4, :].bitcast(I32)
-            queue.dma_start(
-                tile[32 * quadrant : 32 * quadrant + 32, :].bitcast(I32),
-                rows.unsqueeze(0).broadcast_to([8, 4, rows.shape[1]]),
+        def gather(dst, window, first, count):
+            nc.vector.tensor_copy(dst, window[:].indirect(entries(first, count)))
+
+        def permute_words():
+            nc.vector.tensor_copy(
+                w1_w[:].bitcast(I32).rearrange("p (d c i) -> p c d i", d=PACK, i=4),
+                w1_raw_w[:].bitcast(I32).rearrange("p (c i d) -> p c d i", d=PACK, i=4),
             )
 
-        nc.vector.memset(x_s[:].bitcast(I32), 0)
-        nc.vector.memset(w1_raw_s[0:64, :].bitcast(I32), 0)
-        nc.vector.memset(w1_raw_s[64:96, :].bitcast(I32), 0)
-        nc.vector.memset(w_s[0:64, :].bitcast(I32), 0)
-
-        nc.sync.dma_start(offsets[:], offs)
-        for q in range(4):
-            load_scales(nc.sync, x_s, x_scales, q)
-        load_words(nc.sync, w1_raw_w, w1_words)
-        load_words(nc.sync, x_w, x_words)
-        for q in range(3):
-            load_scales(nc.sync, w1_raw_s, w1_scales, q)
-        load_scales_filled(nc.gpsimd, w1_raw_s, w1_scales, 3)
-        load_words(nc.sync, w_w, w_words)
-        for q in range(2):
-            load_scales(nc.sync, w_s, w_scales, q)
-        for q in range(2, 4):
-            load_scales_filled(nc.gpsimd, w_s, w_scales, q)
-
-        banks = [psum.tile([P, BANK], F32, name="bank%d" % b) for b in range(5)]
-
-        def gather_words(dst, first, count):
-            nc.vector.tensor_copy(dst, x_w[:].indirect(entries(first, count)))
-
-        def gather_scales(first, count):
-            nc.vector.tensor_copy(g_s[:, first : first + count], x_s[:].indirect(entries(first, count)))
-
-        def first_layer(c, words, bank):
-            cols = slice(c * CHUNK, (c + 1) * CHUNK)
-            for d in range(PACK):
-                m = slice(d * P, (d + 1) * P)
-                mx(bank[:, m], w1_w[:, m], w1_s[:, m], words, g_s[:, cols])
-            nc.scalar.activation(h_bf[:, cols, :], bank[:].rearrange("p (d j) -> p j d", d=PACK), SILU)
-
-        def quantise(c):
-            cols = slice(c * CHUNK, (c + 1) * CHUNK)
-            nc.vector.quantize_mx(
-                out=h_w[c % 2][:].bitcast(FP8X4), scales=h_s[c % 2][:],
-                in_=h_bf[:, cols, :].rearrange("p j d -> p (j d)"),
-            )
-
-        def second_layer(c, bank, copy):
-            for r in range(2):
-                m = slice(r * P, (r + 1) * P)
-                mx(bank[:, m], w2_w[:, m], w2_s[:, m], h_w[c % 2][:], h_s[c % 2][:])
-            copy(z[:, :, c * CHUNK : (c + 1) * CHUNK], bank[:, 0 : 2 * P].rearrange("p (r j) -> p r j", r=2))
-
-        def light_matmul(r, b, bank):
-            cols = slice(b * BANK, (b + 1) * BANK)
-            m = slice(r * P, (r + 1) * P)
-            mx(bank[:], w_w[:, m], w_s[:, m], x_w[:, cols], x_s[:, cols])
-
-        def light(r, b, bank):
-            light_matmul(r, b, bank)
-            nc.scalar.copy(y[r][:, b * BANK : (b + 1) * BANK], bank[:])
-
-        def scatter(r, first, count):
-            nc.vector.tensor_copy(y[r][:].indirect(entries(first, count)), z[:, r, first : first + count])
-
-        gather_scales(0, S)
-        nc.vector.tensor_copy(
-            w1_w[:].bitcast(I32).rearrange("p (d c i) -> p c d i", d=PACK, i=4),
-            w1_raw_w[:].bitcast(I32).rearrange("p (c i d) -> p c d i", d=PACK, i=4),
-        )
-        load_words(nc.scalar, w2_w, w2_words)
-        for q in range(3):
-            load_scales(nc.scalar, w2_s, w2_scales, q)
-        load_scales(nc.sync, w2_s, w2_scales, 3)
-        gather_words(g_first[:], 0, CHUNK)
-        for half in range(2):
+        def permute_scales(half):
             d = slice(2 * half, 2 * half + 2)
             nc.vector.tensor_copy(
                 w1_s[:].rearrange("p (d c i) -> p c d i", d=PACK, i=16)[:, :, d, :],
                 w1_raw_s[:].rearrange("p (c i d) -> p c d i", d=PACK, i=16)[:, :, d, :],
             )
-        first_layer(0, g_first[:], banks[0])
-        g_rest = keep.tile([P, S - CHUNK], U32, name="g_rest", tag="stage", align_bytes=64)
-        gather_words(g_rest[:, 0:CHUNK], CHUNK, CHUNK)
-        first_layer(1, g_rest[:, 0:CHUNK], banks[1])
-        light(0, 0, banks[2])
+
+        def first_layer(c, bank, words, scales):
+            cols = slice(c * CHUNK, (c + 1) * CHUNK)
+            for d in range(PACK):
+                m = slice(d * P, (d + 1) * P)
+                mx(bank[:, m], w1_w[:, m], w1_s[:, m], words, scales)
+            nc.scalar.activation(h_bf[:, cols, :], bank[:].rearrange("p (d j) -> p j d", d=PACK), SILU)
+
+        def quantise(c):
+            cols = slice(c * CHUNK, (c + 1) * CHUNK)
+            nc.vector.quantize_mx(
+                out=h_w[:, cols].bitcast(FP8X4), scales=h_s[:, cols],
+                in_=h_bf[:, cols, :].rearrange("p j d -> p (j d)"),
+            )
+
+        def second_layer(c, bank, copy):
+            cols = slice(c * CHUNK, (c + 1) * CHUNK)
+            for r in range(2):
+                m = slice(r * P, (r + 1) * P)
+                mx(bank[:, m], w2_w[:, m], w2_s[:, m], h_w[:, cols], h_s[:, cols])
+            copy(z[:, :, cols], bank[:, 0 : 2 * P].rearrange("p (r j) -> p r j", r=2))
+
+        def light(r, b, bank, copy):
+            cols = slice(b * BANK, (b + 1) * BANK)
+            m = slice(r * P, (r + 1) * P)
+            mx(bank[:], w_w[:, m], w_s[:, m], x_w[:, cols], x_s[:, cols])
+            copy(y[r][:, cols], bank[:])
+
+        def scatter(r, first, count):
+            nc.vector.tensor_copy(y[r][:].indirect(entries(first, count)), z[:, r, first : first + count])
+
+        def second_half(c, r, bank, copy):
+            cols = slice(c * CHUNK, (c + 1) * CHUNK)
+            m = slice(r * P, (r + 1) * P)
+            mx(bank[:, 0:CHUNK], w2_w[:, m], w2_s[:, m], h_w[:, cols], h_s[:, cols])
+            copy(z[:, r, cols], bank[:, 0:CHUNK])
+
+        def second_lower(bank):
+            mx(bank[:], w2_w[:, P:], w2_s[:, P:], h_w[:], h_s[:])
+            nc.scalar.copy(z[:, 1, :], bank[:])
+
+        def heavy_first(c, bank):
+            words = g_w0[:] if c == 0 else g_w[:, (c - 1) * CHUNK : c * CHUNK]
+            scales = g_s3[:] if c == 3 else g_s[:, c * CHUNK : (c + 1) * CHUNK]
+            first_layer(c, bank, words, scales)
+
+        nc.vector.memset(x_s[:].bitcast(I32), 0)
+        nc.vector.memset(w1_raw_s[64:96, :].bitcast(I32), 0)
+        nc.vector.memset(w_s[64:96, :].bitcast(I32), 0)
+        nc.vector.memset(warm[:, 0:1], 0.0)
+        nc.sync.dma_start(offsets[:], offs)
+        load_words(nc.sync, w1_raw_w, w1_words)
+        for q in range(4):
+            load_quadrant(nc.sync if q < 2 else nc.scalar, x_s, x_scales, q)
+        load_words(nc.sync, x_w, x_words)
+        nc.scalar.activation(warm[:, 1:2], warm[:, 0:1], SILU)
+        load_three_quadrants(nc.sync, w1_raw_s, w1_scales)
+        load_last_quadrant(nc.gpsimd, w1_raw_s, w1_scales)
+        load_three_quadrants(nc.gpsimd, w_s, w_scales)
+        load_words(nc.sync, w_w, w_words)
+        load_last_quadrant(nc.sync, w_s, w_scales)
+        permute_words()
+        load_words(nc.scalar, w2_w, w2_words)
+        load_quadrant(nc.scalar, w2_s, w2_scales, 3)
+        load_three_quadrants(nc.gpsimd, w2_s, w2_scales)
+
+        gather(g_s[:], x_s, 0, 3 * CHUNK)
+        gather(g_w0[:], x_w, 0, CHUNK)
+        mx(banks[7][:], x_w[:, 0:P], x_s[:, 0:P], x_w[:, 0:BANK], x_s[:, 0:BANK])
+        permute_scales(0)
+        permute_scales(1)
+        heavy_first(0, banks[0])
+        gather(g_w[:, 0:CHUNK], x_w, CHUNK, CHUNK)
+        heavy_first(1, banks[1])
+        gather(g_w[:, CHUNK:], x_w, 2 * CHUNK, 2 * CHUNK)
+        gather(g_s3[:], x_s, 3 * CHUNK, CHUNK)
         quantise(0)
-        gather_words(g_rest[:, CHUNK:], 2 * CHUNK, 2 * CHUNK)
-        light_matmul(0, 1, banks[0])
-        second_layer(0, banks[4], nc.scalar.copy)
+        light(0, 0, banks[2], nc.scalar.copy)
+        light(0, 1, banks[3], nc.vector.tensor_copy)
+        heavy_first(2, banks[0])
         quantise(1)
-        nc.vector.tensor_copy(y[0][:, BANK:], banks[0][:])
-        second_layer(1, banks[3], nc.scalar.copy)
-        first_layer(2, g_rest[:, CHUNK : 2 * CHUNK], banks[1])
+        second_half(0, 0, banks[4], nc.vector.tensor_copy)
+        heavy_first(3, banks[1])
+        second_half(1, 0, banks[5], nc.scalar.copy)
         scatter(0, 0, CHUNK)
-        scatter(0, CHUNK, CHUNK)
-        first_layer(3, g_rest[:, 2 * CHUNK :], banks[4])
         quantise(2)
         quantise(3)
-        light(1, 0, banks[2])
-        light(1, 1, banks[0])
-        second_layer(2, banks[2], nc.scalar.copy)
-        second_layer(3, banks[0], nc.scalar.copy)
-        scatter(1, 0, 2 * CHUNK)
+        second_half(2, 0, banks[2], nc.scalar.copy)
+        second_half(3, 0, banks[3], nc.scalar.copy)
+        scatter(0, CHUNK, CHUNK)
+        light(1, 0, banks[0], nc.scalar.copy)
+        light(1, 1, banks[1], nc.scalar.copy)
+        second_lower(banks[6])
         scatter(0, 2 * CHUNK, 2 * CHUNK)
         nc.sync.dma_start(out[0:P, :], y[0][:])
-        scatter(1, 2 * CHUNK, 2 * CHUNK)
+        scatter(1, 0, S)
         nc.sync.dma_start(out[P : 2 * P, :], y[1][:])

@@ -48,7 +48,7 @@ def tile_moe_cas_mlp_silu_kernel(
         w_w = keep.tile([P, N], U32, name="w_w", align_bytes=64)
         w_s = keep.tile([P, N], U8, name="w_s", align_bytes=64)
         w2_w = w1_raw_w[:, 0:N]
-        w2_s = w1_raw_w[:, N : N + N // PACK].bitcast(U8)
+        w2_s = keep.tile([P, N], U8, name="w2_s", align_bytes=64)
         g_w0 = keep.tile([P, CHUNK], U32, name="g_w0", align_bytes=64)
         g_w = stage.tile([P, 3 * CHUNK], U32, name="g_w", align_bytes=64, offset=0)
         g_s = keep.tile([P, 3 * CHUNK], U8, name="g_s", align_bytes=64)
@@ -150,6 +150,7 @@ def tile_moe_cas_mlp_silu_kernel(
         nc.vector.memset(x_s[:].bitcast(I32), 0)
         nc.vector.memset(w1_raw_s[64:96, :].bitcast(I32), 0)
         nc.vector.memset(w_s[64:96, :].bitcast(I32), 0)
+        nc.vector.memset(w2_s[64:96, :].bitcast(I32), 0)
         nc.vector.memset(warm[:, 0:1], 0.0)
         nc.sync.dma_start(offsets[:], offs)
         load_words(nc.sync, w1_raw_w, w1_words)
@@ -164,7 +165,7 @@ def tile_moe_cas_mlp_silu_kernel(
         load_last_quadrant(nc.sync, w_s, w_scales)
         permute_words()
         load_words(nc.scalar, w2_w, w2_words)
-        load_quadrant(nc.scalar, w2_s, w2_scales, 3)
+        load_last_quadrant(nc.sync, w2_s, w2_scales)
         load_three_quadrants(nc.gpsimd, w2_s, w2_scales)
 
         gather(g_s[:], x_s, 0, 3 * CHUNK)

@@ -107,7 +107,11 @@ def tile_moe_cas_mlp_silu_kernel(
             for d in range(PACK):
                 m = slice(d * P, (d + 1) * P)
                 mx(bank[:, m], w1_w[:, m], w1_s[:, m], words, scales)
-            nc.scalar.activation(h_bf[:, cols, :], bank[:].rearrange("p (d j) -> p j d", d=PACK), SILU)
+            nc.scalar.activation(
+                h_bf[:, cols, :].rearrange("p (c i) d -> p c d i", i=4),
+                bank[:].rearrange("p (d c i) -> p c d i", d=PACK, i=4),
+                SILU,
+            )
 
         def quantise(c):
             cols = slice(c * CHUNK, (c + 1) * CHUNK)
@@ -193,7 +197,7 @@ def tile_moe_cas_mlp_silu_kernel(
         second_half(3, 0, banks[3], nc.scalar.copy)
         scatter(0, CHUNK, CHUNK)
         light(1, 0, banks[0], nc.scalar.copy)
-        light(1, 1, banks[1], nc.scalar.copy)
+        light(1, 1, banks[2], nc.scalar.copy)
         second_lower(banks[6])
         scatter(0, 2 * CHUNK, 2 * CHUNK)
         nc.sync.dma_start(out[0:P, :], y[0][:])

@@ -47,7 +47,7 @@ def tile_moe_cas_mlp_silu_kernel(
         w1_raw_s = stage.tile([P, H], U8, name="w1_raw_s", align_bytes=64, offset=1280)
         w_w = keep.tile([P, N], U32, name="w_w", align_bytes=64)
         w_s = keep.tile([P, N], U8, name="w_s", align_bytes=64)
-        w2_w = w1_raw_w[:, 0:N]
+        w2_w = keep.tile([P, N], U32, name="w2_w", align_bytes=64)
         w2_s = keep.tile([P, N], U8, name="w2_s", align_bytes=64)
         g_w0 = keep.tile([P, CHUNK], U32, name="g_w0", align_bytes=64)
         g_w = stage.tile([P, 3 * CHUNK], U32, name="g_w", align_bytes=64, offset=0)
@@ -159,18 +159,18 @@ def tile_moe_cas_mlp_silu_kernel(
         nc.sync.dma_start(offsets[:], offs)
         load_words(nc.sync, w1_raw_w, w1_words)
         for q in range(4):
-            load_quadrant(nc.sync if q < 2 else nc.scalar, x_s, x_scales, q)
+            load_quadrant(nc.sync, x_s, x_scales, q)
         load_words(nc.sync, x_w, x_words)
         nc.scalar.activation(warm[:, 1:2], warm[:, 0:1], SILU)
         load_three_quadrants(nc.sync, w1_raw_s, w1_scales)
         load_last_quadrant(nc.gpsimd, w1_raw_s, w1_scales)
         load_three_quadrants(nc.gpsimd, w_s, w_scales)
+        load_three_quadrants(nc.gpsimd, w2_s, w2_scales)
         load_words(nc.sync, w_w, w_words)
         load_last_quadrant(nc.sync, w_s, w_scales)
-        permute_words()
-        load_words(nc.scalar, w2_w, w2_words)
+        load_words(nc.sync, w2_w, w2_words)
         load_last_quadrant(nc.sync, w2_s, w2_scales)
-        load_three_quadrants(nc.gpsimd, w2_s, w2_scales)
+        permute_words()
 
         gather(g_s[:], x_s, 0, 3 * CHUNK)
         gather(g_w0[:], x_w, 0, CHUNK)

@@ -154,7 +154,7 @@ def tile_moe_cas_mlp_silu_kernel(
         nc.vector.memset(x_s[:].bitcast(I32), 0)
         nc.vector.memset(w1_raw_s[64:96, :].bitcast(I32), 0)
         nc.vector.memset(w_s[64:96, :].bitcast(I32), 0)
-        nc.vector.memset(w2_s[64:96, :].bitcast(I32), 0)
+        nc.vector.memset(w2_s[64:128, :].bitcast(I32), 0)
         nc.vector.memset(warm[:, 0:1], 0.0)
         nc.sync.dma_start(offsets[:], offs)
         load_words(nc.sync, w1_raw_w, w1_words)
@@ -163,13 +163,13 @@ def tile_moe_cas_mlp_silu_kernel(
         load_words(nc.sync, x_w, x_words)
         nc.scalar.activation(warm[:, 1:2], warm[:, 0:1], SILU)
         load_three_quadrants(nc.sync, w1_raw_s, w1_scales)
-        load_last_quadrant(nc.gpsimd, w1_raw_s, w1_scales)
+        load_last_quadrant(nc.sync, w1_raw_s, w1_scales)
         load_three_quadrants(nc.gpsimd, w_s, w_scales)
         load_three_quadrants(nc.gpsimd, w2_s, w2_scales)
         load_words(nc.sync, w_w, w_words)
         load_last_quadrant(nc.sync, w_s, w_scales)
         load_words(nc.sync, w2_w, w2_words)
-        load_last_quadrant(nc.sync, w2_s, w2_scales)
+        load_quadrant(nc.gpsimd, w2_s, w2_scales, 3)
         permute_words()
 
         gather(g_s[:], x_s, 0, 3 * CHUNK)
@@ -185,19 +185,19 @@ def tile_moe_cas_mlp_silu_kernel(
         quantise(0)
         light(0, 0, banks[2], nc.scalar.copy)
         light(0, 1, banks[3], nc.vector.tensor_copy)
-        heavy_first(2, banks[0])
         quantise(1)
-        second_half(0, 0, banks[4], nc.vector.tensor_copy)
-        heavy_first(3, banks[1])
-        second_half(1, 0, banks[5], nc.scalar.copy)
+        second_half(0, 0, banks[0], nc.scalar.copy)
+        heavy_first(2, banks[1])
+        heavy_first(3, banks[3])
+        second_half(1, 0, banks[2], nc.scalar.copy)
         scatter(0, 0, CHUNK)
         quantise(2)
         quantise(3)
-        second_half(2, 0, banks[2], nc.scalar.copy)
-        second_half(3, 0, banks[3], nc.scalar.copy)
+        second_half(2, 0, banks[4], nc.scalar.copy)
+        second_half(3, 0, banks[5], nc.scalar.copy)
         scatter(0, CHUNK, CHUNK)
-        light(1, 0, banks[0], nc.scalar.copy)
-        light(1, 1, banks[2], nc.scalar.copy)
+        light(1, 0, banks[1], nc.scalar.copy)
+        light(1, 1, banks[3], nc.scalar.copy)
         second_lower(banks[6])
         scatter(0, 2 * CHUNK, 2 * CHUNK)
         nc.sync.dma_start(out[0:P, :], y[0][:])

@@ -53,7 +53,6 @@ def tile_moe_cas_mlp_silu_kernel(
         g_w = stage.tile([P, 3 * CHUNK], U32, name="g_w", align_bytes=64, offset=0)
         g_s = keep.tile([P, 3 * CHUNK], U8, name="g_s", align_bytes=64)
         g_s3 = stage.tile([P, CHUNK], U8, name="g_s3", align_bytes=64, offset=1536)
-        warm = keep.tile([P, 2], F32, name="warm")
 
         def load_words(queue, tile, words):
             queue.dma_start(tile[:].bitcast(I32), words[0].rearrange("p n d -> p (n d)").bitcast(I32))
@@ -154,22 +153,20 @@ def tile_moe_cas_mlp_silu_kernel(
         nc.vector.memset(x_s[:].bitcast(I32), 0)
         nc.vector.memset(w1_raw_s[64:96, :].bitcast(I32), 0)
         nc.vector.memset(w_s[64:96, :].bitcast(I32), 0)
-        nc.vector.memset(w2_s[64:128, :].bitcast(I32), 0)
-        nc.vector.memset(warm[:, 0:1], 0.0)
-        nc.sync.dma_start(offsets[:], offs)
+        nc.vector.memset(w2_s[64:96, :].bitcast(I32), 0)
         load_words(nc.sync, w1_raw_w, w1_words)
+        nc.sync.dma_start(offsets[:], offs)
         for q in range(4):
             load_quadrant(nc.sync, x_s, x_scales, q)
         load_words(nc.sync, x_w, x_words)
-        nc.scalar.activation(warm[:, 1:2], warm[:, 0:1], SILU)
         load_three_quadrants(nc.sync, w1_raw_s, w1_scales)
         load_last_quadrant(nc.sync, w1_raw_s, w1_scales)
-        load_three_quadrants(nc.gpsimd, w_s, w_scales)
-        load_three_quadrants(nc.gpsimd, w2_s, w2_scales)
         load_words(nc.sync, w_w, w_words)
+        load_three_quadrants(nc.sync, w_s, w_scales)
         load_last_quadrant(nc.sync, w_s, w_scales)
         load_words(nc.sync, w2_w, w2_words)
-        load_quadrant(nc.gpsimd, w2_s, w2_scales, 3)
+        load_three_quadrants(nc.sync, w2_s, w2_scales)
+        load_last_quadrant(nc.sync, w2_s, w2_scales)
         permute_words()
 
         gather(g_s[:], x_s, 0, 3 * CHUNK)
@@ -184,12 +181,12 @@ def tile_moe_cas_mlp_silu_kernel(
         gather(g_s3[:], x_s, 3 * CHUNK, CHUNK)
         quantise(0)
         light(0, 0, banks[2], nc.scalar.copy)
-        light(0, 1, banks[3], nc.vector.tensor_copy)
+        light(0, 1, banks[0], nc.vector.tensor_copy)
         quantise(1)
-        second_half(0, 0, banks[0], nc.scalar.copy)
+        second_half(0, 0, banks[3], nc.scalar.copy)
         heavy_first(2, banks[1])
-        heavy_first(3, banks[3])
-        second_half(1, 0, banks[2], nc.scalar.copy)
+        heavy_first(3, banks[2])
+        second_half(1, 0, banks[3], nc.scalar.copy)
         scatter(0, 0, CHUNK)
         quantise(2)
         quantise(3)
@@ -197,7 +194,7 @@ def tile_moe_cas_mlp_silu_kernel(
         second_half(3, 0, banks[5], nc.scalar.copy)
         scatter(0, CHUNK, CHUNK)
         light(1, 0, banks[1], nc.scalar.copy)
-        light(1, 1, banks[3], nc.scalar.copy)
+        light(1, 1, banks[2], nc.scalar.copy)
         second_lower(banks[6])
         scatter(0, 2 * CHUNK, 2 * CHUNK)
         nc.sync.dma_start(out[0:P, :], y[0][:])

@@ -154,8 +154,8 @@ def tile_moe_cas_mlp_silu_kernel(
         nc.vector.memset(w1_raw_s[64:96, :].bitcast(I32), 0)
         nc.vector.memset(w_s[64:96, :].bitcast(I32), 0)
         nc.vector.memset(w2_s[64:96, :].bitcast(I32), 0)
-        load_words(nc.sync, w1_raw_w, w1_words)
         nc.sync.dma_start(offsets[:], offs)
+        load_words(nc.sync, w1_raw_w, w1_words)
         for q in range(4):
             load_quadrant(nc.sync, x_s, x_scales, q)
         load_words(nc.sync, x_w, x_words)
@@ -171,7 +171,6 @@ def tile_moe_cas_mlp_silu_kernel(
 
         gather(g_s[:], x_s, 0, 3 * CHUNK)
         gather(g_w0[:], x_w, 0, CHUNK)
-        mx(banks[7][:], x_w[:, 0:P], x_s[:, 0:P], x_w[:, 0:BANK], x_s[:, 0:BANK])
         permute_scales(0)
         permute_scales(1)
         heavy_first(0, banks[0])

@@ -169,6 +169,8 @@ def tile_moe_cas_mlp_silu_kernel(
         load_last_quadrant(nc.sync, w2_s, w2_scales)
         permute_words()
 
+        for half in range(2):
+            mx(banks[7][0:64, :], w1_raw_w[:, 64 * half : 64 * half + 64], x_s[:, 0:64], w1_raw_w[:], x_s[:, 0:BANK])
         gather(g_s[:], x_s, 0, 3 * CHUNK)
         gather(g_w0[:], x_w, 0, CHUNK)
         permute_scales(0)

@@ -151,22 +151,22 @@ def tile_moe_cas_mlp_silu_kernel(
             first_layer(c, bank, words, scales)
 
         nc.vector.memset(x_s[:].bitcast(I32), 0)
-        nc.vector.memset(w1_raw_s[64:96, :].bitcast(I32), 0)
-        nc.vector.memset(w_s[64:96, :].bitcast(I32), 0)
-        nc.vector.memset(w2_s[64:96, :].bitcast(I32), 0)
+        nc.vector.memset(w1_raw_s[64:128, :].bitcast(I32), 0)
+        nc.vector.memset(w_s[64:128, :].bitcast(I32), 0)
+        nc.vector.memset(w2_s[64:128, :].bitcast(I32), 0)
         nc.sync.dma_start(offsets[:], offs)
         load_words(nc.sync, w1_raw_w, w1_words)
         for q in range(4):
             load_quadrant(nc.sync, x_s, x_scales, q)
         load_words(nc.sync, x_w, x_words)
         load_three_quadrants(nc.sync, w1_raw_s, w1_scales)
-        load_last_quadrant(nc.sync, w1_raw_s, w1_scales)
+        load_quadrant(nc.sync, w1_raw_s, w1_scales, 3)
         load_words(nc.sync, w_w, w_words)
         load_three_quadrants(nc.sync, w_s, w_scales)
-        load_last_quadrant(nc.sync, w_s, w_scales)
+        load_quadrant(nc.sync, w_s, w_scales, 3)
         load_words(nc.sync, w2_w, w2_words)
         load_three_quadrants(nc.sync, w2_s, w2_scales)
-        load_last_quadrant(nc.sync, w2_s, w2_scales)
+        load_quadrant(nc.sync, w2_s, w2_scales, 3)
         permute_words()
 
         for half in range(2):

@@ -20,7 +20,7 @@ CHUNK = 128
 BANK = 512
 LIST_ROWS = 16
 PERIOD = 14
-REPEATS = 5
+REPEATS = 8
 
 
 def tile_moe_cas_mlp_silu_kernel(
@@ -62,19 +62,15 @@ def tile_moe_cas_mlp_silu_kernel(
                 plane[32 * q : 32 * q + 4, :].bitcast(I32), scales[0, 4 * q : 4 * q + 4, :].bitcast(I32)
             )
 
-        def load_three_quadrants(queue, plane, scales):
-            rows = scales[0, 0:PERIOD, :].bitcast(I32)
+        def load_upper_quadrants(queue, plane, scales):
+            rows = scales[0, 2:16, :].bitcast(I32)
             queue.dma_start(
-                plane[0 : PERIOD * REPEATS, :].bitcast(I32),
+                plane[16:128, :].bitcast(I32),
                 rows.unsqueeze(0).broadcast_to([REPEATS, PERIOD, rows.shape[1]]),
             )
 
-        def load_last_quadrant(queue, plane, scales):
-            rows = scales[0, 12:16, :].bitcast(I32)
-            queue.dma_start(
-                plane[96:128, :].bitcast(I32),
-                rows.unsqueeze(0).broadcast_to([8, 4, rows.shape[1]]),
-            )
+        def load_first_quadrant(queue, plane, scales):
+            queue.dma_start(plane[0:16, :].bitcast(I32), scales[0].bitcast(I32))
 
         def mx(dst, lw, ls, rw, rs):
             nc.tensor.matmul_mx(
@@ -151,22 +147,19 @@ def tile_moe_cas_mlp_silu_kernel(
             first_layer(c, bank, words, scales)
 
         nc.vector.memset(x_s[:].bitcast(I32), 0)
-        nc.vector.memset(w1_raw_s[64:128, :].bitcast(I32), 0)
-        nc.vector.memset(w_s[64:128, :].bitcast(I32), 0)
-        nc.vector.memset(w2_s[64:128, :].bitcast(I32), 0)
         nc.sync.dma_start(offsets[:], offs)
         load_words(nc.sync, w1_raw_w, w1_words)
         for q in range(4):
             load_quadrant(nc.sync, x_s, x_scales, q)
         load_words(nc.sync, x_w, x_words)
-        load_three_quadrants(nc.sync, w1_raw_s, w1_scales)
-        load_quadrant(nc.sync, w1_raw_s, w1_scales, 3)
+        load_upper_quadrants(nc.sync, w1_raw_s, w1_scales)
+        load_first_quadrant(nc.sync, w1_raw_s, w1_scales)
         load_words(nc.sync, w_w, w_words)
-        load_three_quadrants(nc.sync, w_s, w_scales)
-        load_quadrant(nc.sync, w_s, w_scales, 3)
+        load_upper_quadrants(nc.sync, w_s, w_scales)
+        load_first_quadrant(nc.sync, w_s, w_scales)
         load_words(nc.sync, w2_w, w2_words)
-        load_three_quadrants(nc.sync, w2_s, w2_scales)
-        load_quadrant(nc.sync, w2_s, w2_scales, 3)
+        load_upper_quadrants(nc.sync, w2_s, w2_scales)
+        load_first_quadrant(nc.sync, w2_s, w2_scales)
         permute_words()
 
         for half in range(2):

@@ -147,13 +147,14 @@ def tile_moe_cas_mlp_silu_kernel(
             first_layer(c, bank, words, scales)
 
         nc.vector.memset(x_s[:].bitcast(I32), 0)
+        nc.vector.memset(w1_raw_s[:].bitcast(I32), 0)
         nc.sync.dma_start(offsets[:], offs)
         load_words(nc.sync, w1_raw_w, w1_words)
         for q in range(4):
             load_quadrant(nc.sync, x_s, x_scales, q)
         load_words(nc.sync, x_w, x_words)
-        load_upper_quadrants(nc.sync, w1_raw_s, w1_scales)
-        load_first_quadrant(nc.sync, w1_raw_s, w1_scales)
+        for q in range(4):
+            load_quadrant(nc.sync, w1_raw_s, w1_scales, q)
         load_words(nc.sync, w_w, w_words)
         load_upper_quadrants(nc.sync, w_s, w_scales)
         load_first_quadrant(nc.sync, w_s, w_scales)

@@ -194,4 +194,5 @@ def tile_moe_cas_mlp_silu_kernel(
         scatter(0, 2 * CHUNK, 2 * CHUNK)
         nc.sync.dma_start(out[0:P, :], y[0][:])
         scatter(1, 0, S)
-        nc.sync.dma_start(out[P : 2 * P, :], y[1][:])
+        for b in range(2):
+            nc.sync.dma_start(out[P : 2 * P, b * BANK : (b + 1) * BANK], y[1][:, b * BANK : (b + 1) * BANK])

@@ -194,5 +194,6 @@ def tile_moe_cas_mlp_silu_kernel(
         scatter(0, 2 * CHUNK, 2 * CHUNK)
         nc.sync.dma_start(out[0:P, :], y[0][:])
         scatter(1, 0, S)
-        for b in range(2):
-            nc.sync.dma_start(out[P : 2 * P, b * BANK : (b + 1) * BANK], y[1][:, b * BANK : (b + 1) * BANK])
+        for b in range(4):
+            cols = slice(b * T // 4, (b + 1) * T // 4)
+            nc.sync.dma_start(out[P : 2 * P, cols], y[1][:, cols])

@@ -32,27 +32,27 @@ def tile_moe_cas_mlp_silu_kernel(
         psum = ctx.enter_context(tc.psum_pool(name="psum", bufs=1))
 
         offsets = keep.tile([P, S // LIST_ROWS], U16, name="offsets")
-        x_w = keep.tile([P, T], U32, name="x_w", align_bytes=64)
-        x_s = keep.tile([P, T], U8, name="x_s", align_bytes=64)
-        w1_raw_w = keep.tile([P, H], U32, name="w1_raw_w", align_bytes=64)
-        w1_w = keep.tile([P, H], U32, name="w1_w", align_bytes=64)
-        w1_s = keep.tile([P, H], U8, name="w1_s", align_bytes=64)
-        h_bf = keep.tile([P, S, PACK], BF16, name="h_bf", align_bytes=64)
-        h_w = keep.tile([P, S], U32, name="h_w", align_bytes=64)
-        h_s = keep.tile([P, S], U8, name="h_s", align_bytes=64)
-        z = keep.tile([P, 2, S], F32, name="z", align_bytes=64)
-        y = [keep.tile([P, T], F32, name="y%d" % r, align_bytes=64) for r in range(2)]
+        x_w = keep.tile([P, T], U32, name="x_w", align_bytes=256)
+        x_s = keep.tile([P, T], U8, name="x_s", align_bytes=256)
+        w1_raw_w = keep.tile([P, H], U32, name="w1_raw_w", align_bytes=256)
+        w1_w = keep.tile([P, H], U32, name="w1_w", align_bytes=256)
+        w1_s = keep.tile([P, H], U8, name="w1_s", align_bytes=256)
+        h_bf = keep.tile([P, S, PACK], BF16, name="h_bf", align_bytes=256)
+        h_w = keep.tile([P, S], U32, name="h_w", align_bytes=256)
+        h_s = keep.tile([P, S], U8, name="h_s", align_bytes=256)
+        z = keep.tile([P, 2, S], F32, name="z", align_bytes=256)
+        y = [keep.tile([P, T], F32, name="y%d" % r, align_bytes=256) for r in range(2)]
         banks = [psum.tile([P, BANK], F32, name="bank%d" % b) for b in range(8)]
         stage = ctx.enter_context(tc.tile_pool(name="stage", bufs=1))
-        w1_raw_s = stage.tile([P, H], U8, name="w1_raw_s", align_bytes=64, offset=1280)
-        w_w = keep.tile([P, N], U32, name="w_w", align_bytes=64)
-        w_s = keep.tile([P, N], U8, name="w_s", align_bytes=64)
-        w2_w = keep.tile([P, N], U32, name="w2_w", align_bytes=64)
-        w2_s = keep.tile([P, N], U8, name="w2_s", align_bytes=64)
-        g_w0 = keep.tile([P, CHUNK], U32, name="g_w0", align_bytes=64)
-        g_w = stage.tile([P, 3 * CHUNK], U32, name="g_w", align_bytes=64, offset=0)
-        g_s = keep.tile([P, 3 * CHUNK], U8, name="g_s", align_bytes=64)
-        g_s3 = stage.tile([P, CHUNK], U8, name="g_s3", align_bytes=64, offset=1536)
+        w1_raw_s = stage.tile([P, H], U8, name="w1_raw_s", align_bytes=256, offset=1280)
+        w_w = keep.tile([P, N], U32, name="w_w", align_bytes=256)
+        w_s = keep.tile([P, N], U8, name="w_s", align_bytes=256)
+        w2_w = keep.tile([P, N], U32, name="w2_w", align_bytes=256)
+        w2_s = keep.tile([P, N], U8, name="w2_s", align_bytes=256)
+        g_w0 = keep.tile([P, CHUNK], U32, name="g_w0", align_bytes=256)
+        g_w = stage.tile([P, 3 * CHUNK], U32, name="g_w", align_bytes=256, offset=0)
+        g_s = keep.tile([P, 3 * CHUNK], U8, name="g_s", align_bytes=256)
+        g_s3 = stage.tile([P, CHUNK], U8, name="g_s3", align_bytes=256, offset=1536)
 
         def load_words(queue, tile, words):
             queue.dma_start(tile[:].bitcast(I32), words[0].rearrange("p n d -> p (n d)").bitcast(I32))

@@ -49,8 +49,8 @@ def tile_moe_cas_mlp_silu_kernel(
         w_s = keep.tile([P, N], U8, name="w_s", align_bytes=256)
         w2_w = keep.tile([P, N], U32, name="w2_w", align_bytes=256)
         w2_s = keep.tile([P, N], U8, name="w2_s", align_bytes=256)
-        g_w0 = keep.tile([P, CHUNK], U32, name="g_w0", align_bytes=256)
-        g_w = stage.tile([P, 3 * CHUNK], U32, name="g_w", align_bytes=256, offset=0)
+        g_w0 = keep.tile([P, 2 * CHUNK], U32, name="g_w0", align_bytes=256)
+        g_w = stage.tile([P, 2 * CHUNK], U32, name="g_w", align_bytes=256, offset=512)
         g_s = keep.tile([P, 3 * CHUNK], U8, name="g_s", align_bytes=256)
         g_s3 = stage.tile([P, CHUNK], U8, name="g_s3", align_bytes=256, offset=1536)
 
@@ -91,7 +91,7 @@ def tile_moe_cas_mlp_silu_kernel(
             )
 
         def permute_scales(half):
-            d = slice(2 * half, 2 * half + 2)
+            d = slice(half, half + 1)
             nc.vector.tensor_copy(
                 w1_s[:].rearrange("p (d c i) -> p c d i", d=PACK, i=16)[:, :, d, :],
                 w1_raw_s[:].rearrange("p (c i d) -> p c d i", d=PACK, i=16)[:, :, d, :],
@@ -142,7 +142,7 @@ def tile_moe_cas_mlp_silu_kernel(
             nc.scalar.copy(z[:, 1, :], bank[:])
 
         def heavy_first(c, bank):
-            words = g_w0[:] if c == 0 else g_w[:, (c - 1) * CHUNK : c * CHUNK]
+            words = (g_w0, g_w)[c // 2][:, c % 2 * CHUNK : (c % 2 + 1) * CHUNK]
             scales = g_s3[:] if c == 3 else g_s[:, c * CHUNK : (c + 1) * CHUNK]
             first_layer(c, bank, words, scales)
 
@@ -155,8 +155,8 @@ def tile_moe_cas_mlp_silu_kernel(
         load_words(nc.sync, x_w, x_words)
         for q in range(4):
             load_quadrant(nc.sync, w1_raw_s, w1_scales, q)
-        load_words(nc.sync, w_w, w_words)
         load_upper_quadrants(nc.sync, w_s, w_scales)
+        load_words(nc.sync, w_w, w_words)
         load_first_quadrant(nc.sync, w_s, w_scales)
         load_words(nc.sync, w2_w, w2_words)
         load_upper_quadrants(nc.sync, w2_s, w2_scales)
@@ -166,13 +166,13 @@ def tile_moe_cas_mlp_silu_kernel(
         for half in range(2):
             mx(banks[7][0:64, :], w1_raw_w[:, 64 * half : 64 * half + 64], x_s[:, 0:64], w1_raw_w[:], x_s[:, 0:BANK])
         gather(g_s[:], x_s, 0, 3 * CHUNK)
-        gather(g_w0[:], x_w, 0, CHUNK)
-        permute_scales(0)
-        permute_scales(1)
+        gather(g_w0[:, 0:CHUNK], x_w, 0, CHUNK)
+        gather(g_w0[:, CHUNK:], x_w, CHUNK, CHUNK)
+        for d in range(PACK):
+            permute_scales(d)
         heavy_first(0, banks[0])
-        gather(g_w[:, 0:CHUNK], x_w, CHUNK, CHUNK)
         heavy_first(1, banks[1])
-        gather(g_w[:, CHUNK:], x_w, 2 * CHUNK, 2 * CHUNK)
+        gather(g_w[:], x_w, 2 * CHUNK, 2 * CHUNK)
         gather(g_s3[:], x_s, 3 * CHUNK, CHUNK)
         quantise(0)
         light(0, 0, banks[2], nc.scalar.copy)

from contextlib import ExitStack

import concourse.mybir as mybir

K, T, S, H, N = 512, 1024, 512, 512, 256
FLOPS = 2 * K * N * T + 2 * K * H * S + 2 * H * N * S

F32 = mybir.dt.float32
BF16 = mybir.dt.bfloat16
I32 = mybir.dt.int32
U32 = mybir.dt.uint32
U16 = mybir.dt.uint16
U8 = mybir.dt.uint8
FP8X4 = mybir.dt.float8_e4m3fn_x4
SILU = mybir.ActivationFunctionType.Silu

P = 128
PACK = 4
CHUNK = 128
BANK = 512
LIST_ROWS = 16
PERIOD = 14
REPEATS = 8


def tile_moe_cas_mlp_silu_kernel(
    tc, x_words, x_scales, w_words, w_scales, w1_words, w1_scales, w2_words, w2_scales, offs, out
):
    nc = tc.nc
    with ExitStack() as ctx:
        keep = ctx.enter_context(tc.tile_pool(name="keep", bufs=1))
        psum = ctx.enter_context(tc.psum_pool(name="psum", bufs=1))

        offsets = keep.tile([P, S // LIST_ROWS], U16, name="offsets")
        x_w = keep.tile([P, T], U32, name="x_w", align_bytes=256)
        x_s = keep.tile([P, T], U8, name="x_s", align_bytes=256)
        w1_raw_w = keep.tile([P, H], U32, name="w1_raw_w", align_bytes=256)
        w1_w = keep.tile([P, H], U32, name="w1_w", align_bytes=256)
        w1_s = keep.tile([P, H], U8, name="w1_s", align_bytes=256)
        h_bf = keep.tile([P, S, PACK], BF16, name="h_bf", align_bytes=256)
        h_w = keep.tile([P, S], U32, name="h_w", align_bytes=256)
        h_s = keep.tile([P, S], U8, name="h_s", align_bytes=256)
        z = keep.tile([P, 2, S], F32, name="z", align_bytes=256)
        y = [keep.tile([P, T], F32, name="y%d" % r, align_bytes=256) for r in range(2)]
        banks = [psum.tile([P, BANK], F32, name="bank%d" % b) for b in range(8)]
        stage = ctx.enter_context(tc.tile_pool(name="stage", bufs=1))
        w1_raw_s = stage.tile([P, H], U8, name="w1_raw_s", align_bytes=256, offset=1280)
        w_w = keep.tile([P, N], U32, name="w_w", align_bytes=256)
        w_s = keep.tile([P, N], U8, name="w_s", align_bytes=256)
        w2_w = keep.tile([P, N], U32, name="w2_w", align_bytes=256)
        w2_s = keep.tile([P, N], U8, name="w2_s", align_bytes=256)
        g_w0 = keep.tile([P, 2 * CHUNK], U32, name="g_w0", align_bytes=256)
        g_w = stage.tile([P, 2 * CHUNK], U32, name="g_w", align_bytes=256, offset=512)
        g_s = keep.tile([P, 3 * CHUNK], U8, name="g_s", align_bytes=256)
        g_s3 = stage.tile([P, CHUNK], U8, name="g_s3", align_bytes=256, offset=1536)

        def load_words(queue, tile, words):
            queue.dma_start(tile[:].bitcast(I32), words[0].rearrange("p n d -> p (n d)").bitcast(I32))

        def load_quadrant(queue, plane, scales, q):
            queue.dma_start(
                plane[32 * q : 32 * q + 4, :].bitcast(I32), scales[0, 4 * q : 4 * q + 4, :].bitcast(I32)
            )

        def load_upper_quadrants(queue, plane, scales):
            rows = scales[0, 2:16, :].bitcast(I32)
            queue.dma_start(
                plane[16:128, :].bitcast(I32),
                rows.unsqueeze(0).broadcast_to([REPEATS, PERIOD, rows.shape[1]]),
            )

        def load_first_quadrant(queue, plane, scales):
            queue.dma_start(plane[0:16, :].bitcast(I32), scales[0].bitcast(I32))

        def mx(dst, lw, ls, rw, rs):
            nc.tensor.matmul_mx(
                out=dst, lhsT=lw.bitcast(FP8X4), lhsT_scale=ls, rhs=rw.bitcast(FP8X4), rhs_scale=rs,
                start=True, stop=True,
            )

        def entries(first, count):
            return offsets[:, first // LIST_ROWS : (first + count) // LIST_ROWS]

        def gather(dst, window, first, count):
            nc.vector.tensor_copy(dst, window[:].indirect(entries(first, count)))

        def permute_words():
            nc.vector.tensor_copy(
                w1_w[:].bitcast(I32).rearrange("p (d c i) -> p c d i", d=PACK, i=4),
                w1_raw_w[:].bitcast(I32).rearrange("p (c i d) -> p c d i", d=PACK, i=4),
            )

        def permute_scales(half):
            d = slice(half, half + 1)
            nc.vector.tensor_copy(
                w1_s[:].rearrange("p (d c i) -> p c d i", d=PACK, i=16)[:, :, d, :],
                w1_raw_s[:].rearrange("p (c i d) -> p c d i", d=PACK, i=16)[:, :, d, :],
            )

        def first_layer(c, bank, words, scales):
            cols = slice(c * CHUNK, (c + 1) * CHUNK)
            for d in range(PACK):
                m = slice(d * P, (d + 1) * P)
                mx(bank[:, m], w1_w[:, m], w1_s[:, m], words, scales)
            nc.scalar.activation(
                h_bf[:, cols, :].rearrange("p (c i) d -> p c d i", i=4),
                bank[:].rearrange("p (d c i) -> p c d i", d=PACK, i=4),
                SILU,
            )

        def quantise(c):
            cols = slice(c * CHUNK, (c + 1) * CHUNK)
            nc.vector.quantize_mx(
                out=h_w[:, cols].bitcast(FP8X4), scales=h_s[:, cols],
                in_=h_bf[:, cols, :].rearrange("p j d -> p (j d)"),
            )

        def second_layer(c, bank, copy):
            cols = slice(c * CHUNK, (c + 1) * CHUNK)
            for r in range(2):
                m = slice(r * P, (r + 1) * P)
                mx(bank[:, m], w2_w[:, m], w2_s[:, m], h_w[:, cols], h_s[:, cols])
            copy(z[:, :, cols], bank[:, 0 : 2 * P].rearrange("p (r j) -> p r j", r=2))

        def light(r, b, bank, copy):
            cols = slice(b * BANK, (b + 1) * BANK)
            m = slice(r * P, (r + 1) * P)
            mx(bank[:], w_w[:, m], w_s[:, m], x_w[:, cols], x_s[:, cols])
            copy(y[r][:, cols], bank[:])

        def scatter(r, first, count):
            nc.vector.tensor_copy(y[r][:].indirect(entries(first, count)), z[:, r, first : first + count])

        def second_half(c, r, bank, copy):
            cols = slice(c * CHUNK, (c + 1) * CHUNK)
            m = slice(r * P, (r + 1) * P)
            mx(bank[:, 0:CHUNK], w2_w[:, m], w2_s[:, m], h_w[:, cols], h_s[:, cols])
            copy(z[:, r, cols], bank[:, 0:CHUNK])

        def second_lower(bank):
            mx(bank[:], w2_w[:, P:], w2_s[:, P:], h_w[:], h_s[:])
            nc.scalar.copy(z[:, 1, :], bank[:])

        def heavy_first(c, bank):
            words = (g_w0, g_w)[c // 2][:, c % 2 * CHUNK : (c % 2 + 1) * CHUNK]
            scales = g_s3[:] if c == 3 else g_s[:, c * CHUNK : (c + 1) * CHUNK]
            first_layer(c, bank, words, scales)

        nc.vector.memset(x_s[:].bitcast(I32), 0)
        nc.vector.memset(w1_raw_s[:].bitcast(I32), 0)
        nc.sync.dma_start(offsets[:], offs)
        load_words(nc.sync, w1_raw_w, w1_words)
        for q in range(4):
            load_quadrant(nc.sync, x_s, x_scales, q)
        load_words(nc.sync, x_w, x_words)
        for q in range(4):
            load_quadrant(nc.sync, w1_raw_s, w1_scales, q)
        load_upper_quadrants(nc.sync, w_s, w_scales)
        load_words(nc.sync, w_w, w_words)
        load_first_quadrant(nc.sync, w_s, w_scales)
        load_words(nc.sync, w2_w, w2_words)
        load_upper_quadrants(nc.sync, w2_s, w2_scales)
        load_first_quadrant(nc.sync, w2_s, w2_scales)
        permute_words()

        for half in range(2):
            mx(banks[7][0:64, :], w1_raw_w[:, 64 * half : 64 * half + 64], x_s[:, 0:64], w1_raw_w[:], x_s[:, 0:BANK])
        gather(g_s[:], x_s, 0, 3 * CHUNK)
        gather(g_w0[:, 0:CHUNK], x_w, 0, CHUNK)
        gather(g_w0[:, CHUNK:], x_w, CHUNK, CHUNK)
        for d in range(PACK):
            permute_scales(d)
        heavy_first(0, banks[0])
        heavy_first(1, banks[1])
        gather(g_w[:], x_w, 2 * CHUNK, 2 * CHUNK)
        gather(g_s3[:], x_s, 3 * CHUNK, CHUNK)
        quantise(0)
        light(0, 0, banks[2], nc.scalar.copy)
        light(0, 1, banks[0], nc.vector.tensor_copy)
        quantise(1)
        second_half(0, 0, banks[3], nc.scalar.copy)
        heavy_first(2, banks[1])
        heavy_first(3, banks[2])
        second_half(1, 0, banks[3], nc.scalar.copy)
        scatter(0, 0, CHUNK)
        quantise(2)
        quantise(3)
        second_half(2, 0, banks[4], nc.scalar.copy)
        second_half(3, 0, banks[5], nc.scalar.copy)
        scatter(0, CHUNK, CHUNK)
        light(1, 0, banks[1], nc.scalar.copy)
        light(1, 1, banks[2], nc.scalar.copy)
        second_lower(banks[6])
        scatter(0, 2 * CHUNK, 2 * CHUNK)
        nc.sync.dma_start(out[0:P, :], y[0][:])
        scatter(1, 0, S)
        for b in range(4):
            cols = slice(b * T // 4, (b + 1) * T // 4)
            nc.sync.dma_start(out[P : 2 * P, cols], y[1][:, cols])
